import numpy as np, ml_dtypes
CORES = [66,70,74,78,82,86,90,94,98,102,106,110,114,118,122,126]
N = 16
DEG, TK = 4, 256
MASK = [[0,1,8,12],[1,3,8,12],[2,7,10,13],[2,3,5,13],[4,6,8,15],[4,5,11,13],[6,9,14,15],[1,3,5,7],[6,8,9,13],[9,11,12,15],[6,7,10,13],[2,5,11,14],[1,7,8,12],[1,10,12,13],[6,12,13,14],[5,8,12,15]]
def setup_inputs(rng):
    return {"x": rng.standard_normal((N, 128, TK), dtype=np.float32).astype(ml_dtypes.bfloat16), "w": rng.standard_normal((N, 128, DEG * 128), dtype=np.float32).astype(ml_dtypes.bfloat16)}
def setup_inputs_big(rng):
    d = setup_inputs(rng)
    for k in ("x", "w"): d[k] = (d[k].astype(np.float32) * 1024.0).astype(d[k].dtype)
    return d
def setup_inputs_small(rng):
    d = setup_inputs(rng)
    for k in ("x", "w"): d[k] = (d[k].astype(np.float32) * (1 / 1024.0)).astype(d[k].dtype)
    return d
def setup_inputs_apart(rng):
    d = setup_inputs(rng)
    f = (10.0 ** rng.permutation(np.linspace(-1.5, 1.5, N))).astype(np.float32).reshape(N, 1, 1)
    for k in ("x", "w"): d[k] = (d[k].astype(np.float32) * f).astype(d[k].dtype)
    return d
def reference(x, w):
    X, W = x.astype(np.float64), w.astype(np.float64)
    y = np.zeros((N, 128, TK))
    for r in range(N):
        for i, j in enumerate(MASK[r]):
            y[r] += W[r][:, 128 * i:128 * i + 128].T @ X[j]
    return {"y": y.astype(ml_dtypes.bfloat16 if x.dtype != np.float64 else np.float64)}

@@ -1,0 +1,175 @@
+from concourse.bass import DstId, RemoteDMATransfer
+
+N = 16
+TK = 256
+TM = 128
+DEG = 4
+CAP = 4
+
+SCRATCH = {
+    "x0": ("sbuf", [128, TK], "bfloat16"),
+    "x1": ("sbuf", [128, TK], "bfloat16"),
+    "x2": ("sbuf", [128, TK], "bfloat16"),
+    "x3": ("sbuf", [128, TK], "bfloat16"),
+    "wsb": ("sbuf", [128, DEG * TM], "bfloat16"),
+    "ysb": ("sbuf", [128, TK], "bfloat16"),
+    "acc": ("psum", [128, TK], "float32"),
+}
+SEMAPHORES = ["xl", "wl", "mm", "cp", "st", "sent"] + ["a%d" % j for j in range(N)]
+
+
+def _bits(m):
+    return bin(m).count("1")
+
+
+def make_plan(cores, MASK, topo):
+    n = len(cores)
+
+    def chip(r):
+        return topo.chip(cores[r])
+
+    def near(a, b):
+        return topo.mates(chip(a), chip(b)) or topo.same_plane(chip(a), chip(b))
+
+    recv = [[r for r in range(n) if j in MASK[r] and r != j] for j in range(n)]
+    off = [[r for r in recv[j] if chip(r) != chip(j)] for j in range(n)]
+    on = [[r for r in recv[j] if chip(r) == chip(j)] for j in range(n)]
+    work = [len(off[j]) for j in range(n)]
+    kids = {}
+    for j in sorted(range(n), key=lambda s: -len(off[s])):
+        while len(off[j]) > CAP:
+            best = None
+            for h in off[j]:
+                if not recv[h]:
+                    continue
+                for d in off[j]:
+                    if d == h or (d, j) in kids or not topo.may_write(cores[h], cores[d]):
+                        continue
+                    same = chip(h) == chip(d)
+                    if not (same or near(h, d)):
+                        continue
+                    key = (0 if same else 1, work[h], 1 if near(j, d) else 0, h, d)
+                    if best is None or key < best:
+                        best = key
+            if best is None:
+                break
+            h, d = best[3], best[4]
+            kids.setdefault((h, j), []).append(d)
+            off[j].remove(d)
+            work[j] -= 1
+            if chip(h) != chip(d):
+                work[h] += 1
+
+    calls = [[] for _ in range(n)]
+    arrive = [{} for _ in range(n)]
+    HOP = 2.0
+    relays = [[] for _ in range(n)]
+    for j in range(n):
+        heads = sorted([r for r in off[j] if (r, j) in kids], key=lambda r: -len(kids[(r, j)]))
+        rest = [r for r in off[j] if (r, j) not in kids]
+        order, used = list(heads), {True: 0, False: 0}
+        for r in heads:
+            used[topo.same_plane(chip(j), chip(r))] += 1
+        while rest:
+            r = min(rest, key=lambda q: (used[topo.same_plane(chip(j), chip(q))], q))
+            rest.remove(r)
+            order.append(r)
+            used[topo.same_plane(chip(j), chip(r))] += 1
+        if order:
+            calls[j].append((None, [("off", j, order)]))
+        if on[j]:
+            calls[j].append((None, [("on", j, list(on[j]))]))
+        for p, r in enumerate(order):
+            arrive[r][j] = 1.0 + p
+        for p, r in enumerate(on[j]):
+            arrive[r][j] = 1.5 + p
+        for h in heads:
+            far = [d for d in kids[(h, j)] if chip(d) != chip(h)]
+            loc = [d for d in kids[(h, j)] if chip(d) == chip(h)]
+            grp = "on" if on[h] else "off"
+            trs = []
+            if grp == "off" and far and loc:
+                trs.append(("off", j, far + loc))
+            else:
+                if far:
+                    trs.append(("off", j, far))
+                if loc:
+                    trs.append((grp, j, loc))
+            relays[h].append((arrive[h][j], j, trs))
+            for _, _, ds in trs:
+                for p, d in enumerate(ds):
+                    arrive[d][j] = arrive[h][j] + HOP + 1.0 + p
+    for h in range(n):
+        for _, j, trs in sorted(relays[h]):
+            calls[h].append((j, trs))
+    return calls, arrive
+
+
+def rank_program(g, core, T, topo):
+    rank = T.rank_of(core)
+    if rank is None:
+        return
+    cores, MASK = T.cores, T.tables["MASK"]
+    calls, arrive = make_plan(cores, MASK, topo)
+
+    def groups(c):
+        full, low = 0, None
+        for d in cores:
+            if d != c:
+                m = topo.mask(c, d)
+                full |= m
+                low = m if low is None else (low & m)
+        return {"off": low, "on": (full & ~low) or low}
+
+    def slot(r, j):
+        return T["x%d" % MASK[r].index(j)]
+
+    need = {}
+    for s in range(len(cores)):
+        gs = groups(cores[s])
+        for _, trs in calls[s]:
+            for grp, j, ds in trs:
+                if rank in ds:
+                    need[j] = _bits(gs[grp])
+
+    g.sync.dma_start(slot(rank, rank)[:, :], T.x[:, :]).then_inc(T.sem.xl, 16)
+    g.sync.dma_start(T.wsb[:, :], T.w[:, :]).then_inc(T.sem.wl, 16)
+
+    mine = groups(core)
+    sent = 0
+    if calls[rank]:
+        g.wait_ge(T.sem.xl, 16)
+    for waited, trs in calls[rank]:
+        if waited is not None:
+            g.wait_ge(T.sem["a%d" % waited], need[waited])
+        lst = []
+        for grp, j, ds in trs:
+            ids = []
+            for d in ds:
+                rid, pid, _ = topo.addr(cores[d])
+                ids.append(DstId(rid=rid, pnc=pid))
+            lst.append(RemoteDMATransfer(dst_ids=ids, dma_engine_mask=mine[grp], remote_sem=T.sem["a%d" % j],
+                                         srcs=[slot(rank, j)[:, :]], dsts=[slot(d, j)[:, :] for d in ds], alu_op=0))
+            sent += _bits(mine[grp])
+        g.remote_dma_fused(lst, local_sem=T.sem.sent)
+
+    order = sorted(range(DEG), key=lambda i: (arrive[rank].get(MASK[rank][i], 0.0), i))
+    g.tensor.wait_ge(T.sem.wl, 16)
+    last = None
+    for k, i in enumerate(order):
+        j = MASK[rank][i]
+        if j == rank:
+            g.tensor.wait_ge(T.sem.xl, 16)
+        else:
+            g.tensor.wait_ge(T.sem["a%d" % j], need[j])
+        last = g.tensor.matmul(T.acc[:, :], T.wsb[:, TM * i:TM * (i + 1)], T["x%d" % i][:, :], k == 0, k == DEG - 1)
+    last.then_inc(T.sem.mm, 1)
+
+    g.vector.wait_ge(T.sem.mm, 1)
+    g.vector.tensor_copy(T.ysb[:, :], T.acc[:, :]).then_inc(T.sem.cp, 1)
+
+    g.sync.wait_ge(T.sem.cp, 1)
+    g.sync.dma_start(T.y[:, :], T.ysb[:, :]).then_inc(T.sem.st, 16)
+    g.sync.wait_ge(T.sem.st, 16)
+    if sent:
+        g.wait_ge(T.sem.sent, sent)

@@ -1,107 +1,101 @@
 from concourse.bass import DstId, RemoteDMATransfer
+from concourse.mybir import ActivationFunctionType
 
 N = 16
 TK = 256
+TH = TK // 2
 TM = 128
 DEG = 4
-CAP = 4
 
 SCRATCH = {
     "x0": ("sbuf", [128, TK], "bfloat16"),
     "x1": ("sbuf", [128, TK], "bfloat16"),
     "x2": ("sbuf", [128, TK], "bfloat16"),
     "x3": ("sbuf", [128, TK], "bfloat16"),
+    "hx": ("sbuf", [128, TK], "bfloat16"),
+    "xd": ("dram", [128, TK], "bfloat16"),
     "wsb": ("sbuf", [128, DEG * TM], "bfloat16"),
     "ysb": ("sbuf", [128, TK], "bfloat16"),
-    "acc": ("psum", [128, TK], "float32"),
+    "acc0": ("psum", [128, 512], "float32"),
+    "acc1": ("psum", [128, 512], "float32"),
 }
-SEMAPHORES = ["xl", "wl", "mm", "cp", "st", "sent"] + ["a%d" % j for j in range(N)]
+SEMAPHORES = ["xl", "xs", "wl", "m0", "m1", "c0", "c1", "st", "sent"] + ["a%d" % j for j in range(N)]
+
+ROUTES = {
+    1: [(None, [("ports", 1, [7, 12, 13])]), (None, [("in", 1, [0])]), (8, [("in", 8, [0])])],
+    2: [(None, [("off", 2, [11])]), (None, [("in", 2, [3])]), (13, [("all", 13, [3])])],
+    3: [(None, [("ports", 3, [1, 7])])],
+    4: [(None, [("off", 4, [5])]), (5, [("off", 5, [3])])],
+    5: [(None, [("in", 5, [4])]), (None, [("off", 5, [7, 11, 15])])],
+    6: [(None, [("ports", 6, [4, 8, 10, 14])])],
+    7: [(None, [("ports", 7, [2, 10, 12])])],
+    8: [(None, [("off", 8, [1, 4])]), (None, [("side", 8, [15, 12])])],
+    9: [(None, [("off", 9, [6])]), (None, [("in", 9, [8])])],
+    10: [(None, [("ports", 10, [2, 13])])],
+    11: [(None, [("ports", 11, [5, 9])])],
+    12: [(None, [("off", 12, [15, 0])]), (None, [("side", 12, [1, 9])]), (None, [("in", 12, [13])])],
+    13: [(None, [("off", 13, [14, 2])]), (None, [("side", 13, [5, 8])])],
+    14: [(None, [("off", 14, [6, 11])]), (13, [("off", 13, [10])])],
+    15: [(None, [("ports", 15, [6, 4, 9])]), (12, [("in", 12, [14])])],
+}
 
 
 def _bits(m):
     return bin(m).count("1")
 
 
-def make_plan(cores, MASK, topo):
+def make_plan(cores, topo):
     n = len(cores)
 
     def chip(r):
         return topo.chip(cores[r])
 
-    def near(a, b):
-        return topo.mates(chip(a), chip(b)) or topo.same_plane(chip(a), chip(b))
-
-    recv = [[r for r in range(n) if j in MASK[r] and r != j] for j in range(n)]
-    off = [[r for r in recv[j] if chip(r) != chip(j)] for j in range(n)]
-    on = [[r for r in recv[j] if chip(r) == chip(j)] for j in range(n)]
-    work = [len(off[j]) for j in range(n)]
-    kids = {}
-    for j in sorted(range(n), key=lambda s: -len(off[s])):
-        while len(off[j]) > CAP:
-            best = None
-            for h in off[j]:
-                if not recv[h]:
-                    continue
-                for d in off[j]:
-                    if d == h or (d, j) in kids or not topo.may_write(cores[h], cores[d]):
-                        continue
-                    same = chip(h) == chip(d)
-                    if not (same or near(h, d)):
-                        continue
-                    key = (0 if same else 1, work[h], 1 if near(j, d) else 0, h, d)
-                    if best is None or key < best:
-                        best = key
-            if best is None:
-                break
-            h, d = best[3], best[4]
-            kids.setdefault((h, j), []).append(d)
-            off[j].remove(d)
-            work[j] -= 1
-            if chip(h) != chip(d):
-                work[h] += 1
-
     calls = [[] for _ in range(n)]
+    for r in range(n):
+        for waited, trs in ROUTES.get(r, []):
+            out = []
+            for how, j, ds in trs:
+                if how == "ports":
+                    s = [d for d in ds if topo.same_plane(chip(r), chip(d))]
+                    m = [d for d in ds if d not in s]
+                    while len(m) > len(s) + 1:
+                        s.append(m.pop())
+                    while len(s) > len(m) + 1:
+                        m.append(s.pop())
+                    if m and s:
+                        out += [("A", j, m), ("B", j, s)]
+                    else:
+                        out.append(("O", j, list(ds)))
+                elif how == "side":
+                    out += [("A", j, [ds[0]]), ("B", j, [ds[1]])]
+                else:
+                    out.append(({"off": "O", "in": "I", "all": "F"}[how], j, list(ds)))
+            calls[r].append((waited, out))
+
+    parts = {"O": "AB", "A": "A", "B": "B", "I": "I", "F": "ABI"}
+    dur = {"O": 1.0, "A": 2.0, "B": 2.0, "I": 1.0, "F": 0.5}
     arrive = [{} for _ in range(n)]
-    HOP = 2.0
-    relays = [[] for _ in range(n)]
-    for j in range(n):
-        heads = sorted([r for r in off[j] if (r, j) in kids], key=lambda r: -len(kids[(r, j)]))
-        rest = [r for r in off[j] if (r, j) not in kids]
-        order, used = list(heads), {True: 0, False: 0}
-        for r in heads:
-            used[topo.same_plane(chip(j), chip(r))] += 1
-        while rest:
-            r = min(rest, key=lambda q: (used[topo.same_plane(chip(j), chip(q))], q))
-            rest.remove(r)
-            order.append(r)
-            used[topo.same_plane(chip(j), chip(r))] += 1
-        if order:
-            calls[j].append((None, [("off", j, order)]))
-        if on[j]:
-            calls[j].append((None, [("on", j, list(on[j]))]))
-        for p, r in enumerate(order):
-            arrive[r][j] = 1.0 + p
-        for p, r in enumerate(on[j]):
-            arrive[r][j] = 1.5 + p
-        for h in heads:
-            far = [d for d in kids[(h, j)] if chip(d) != chip(h)]
-            loc = [d for d in kids[(h, j)] if chip(d) == chip(h)]
-            grp = "on" if on[h] else "off"
-            trs = []
-            if grp == "off" and far and loc:
-                trs.append(("off", j, far + loc))
-            else:
-                if far:
-                    trs.append(("off", j, far))
-                if loc:
-                    trs.append((grp, j, loc))
-            relays[h].append((arrive[h][j], j, trs))
-            for _, _, ds in trs:
-                for p, d in enumerate(ds):
-                    arrive[d][j] = arrive[h][j] + HOP + 1.0 + p
-    for h in range(n):
-        for _, j, trs in sorted(relays[h]):
-            calls[h].append((j, trs))
+    free = [{"A": 0.0, "B": 0.0, "I": 0.0} for _ in range(n)]
+    at, clock = [0] * n, [0.0] * n
+    moved = True
+    while moved:
+        moved = False
+        for r in range(n):
+            while at[r] < len(calls[r]):
+                waited, trs = calls[r][at[r]]
+                if waited is not None and waited not in arrive[r]:
+                    break
+                t0 = clock[r] + 0.3 if waited is None else max(clock[r] + 0.3, arrive[r][waited] + 2.0)
+                clock[r] = t0
+                for grp, j, ds in trs:
+                    t = max([t0] + [free[r][p] for p in parts[grp]])
+                    for d in ds:
+                        t += dur[grp]
+                        arrive[d][j] = t
+                    for p in parts[grp]:
+                        free[r][p] = t
+                at[r] += 1
+                moved = True
     return calls, arrive
 
 
@@ -110,7 +104,7 @@ def rank_program(g, core, T, topo):
     if rank is None:
         return
     cores, MASK = T.cores, T.tables["MASK"]
-    calls, arrive = make_plan(cores, MASK, topo)
+    calls, arrive = make_plan(cores, topo)
 
     def groups(c):
         full, low = 0, None
@@ -119,10 +113,12 @@ def rank_program(g, core, T, topo):
                 m = topo.mask(c, d)
                 full |= m
                 low = m if low is None else (low & m)
-        return {"off": low, "on": (full & ~low) or low}
+        bits = [b for b in range(full.bit_length()) if (low >> b) & 1]
+        a = sum(1 << b for b in bits[:len(bits) // 2])
+        return {"O": low, "A": a, "B": low & ~a, "I": full & ~low, "F": full}
 
     def slot(r, j):
-        return T["x%d" % MASK[r].index(j)]
+        return T["x%d" % MASK[r].index(j)] if j in MASK[r] else T.hx
 
     need = {}
     for s in range(len(cores)):
@@ -132,8 +128,10 @@ def rank_program(g, core, T, topo):
                 if rank in ds:
                     need[j] = _bits(gs[grp])
 
-    g.sync.dma_start(slot(rank, rank)[:, :], T.x[:, :]).then_inc(T.sem.xl, 16)
+    if calls[rank]:
+        g.sync.dma_start(T.xd[:, :], T.x[:, :]).then_inc(T.sem.xl, 16)
     g.sync.dma_start(T.wsb[:, :], T.w[:, :]).then_inc(T.sem.wl, 16)
+    g.sync.dma_start(slot(rank, rank)[:, :], T.x[:, :]).then_inc(T.sem.xs, 16)
 
     mine = groups(core)
     sent = 0
@@ -148,27 +146,34 @@ def rank_program(g, core, T, topo):
             for d in ds:
                 rid, pid, _ = topo.addr(cores[d])
                 ids.append(DstId(rid=rid, pnc=pid))
+            src = T.xd if j == rank else slot(rank, j)
             lst.append(RemoteDMATransfer(dst_ids=ids, dma_engine_mask=mine[grp], remote_sem=T.sem["a%d" % j],
-                                         srcs=[slot(rank, j)[:, :]], dsts=[slot(d, j)[:, :] for d in ds], alu_op=0))
+                                         srcs=[src[:, :]], dsts=[slot(d, j)[:, :] for d in ds], alu_op=0))
             sent += _bits(mine[grp])
         g.remote_dma_fused(lst, local_sem=T.sem.sent)
 
     order = sorted(range(DEG), key=lambda i: (arrive[rank].get(MASK[rank][i], 0.0), i))
     g.tensor.wait_ge(T.sem.wl, 16)
-    last = None
     for k, i in enumerate(order):
         j = MASK[rank][i]
         if j == rank:
-            g.tensor.wait_ge(T.sem.xl, 16)
+            g.tensor.wait_ge(T.sem.xs, 16)
         else:
             g.tensor.wait_ge(T.sem["a%d" % j], need[j])
-        last = g.tensor.matmul(T.acc[:, :], T.wsb[:, TM * i:TM * (i + 1)], T["x%d" % i][:, :], k == 0, k == DEG - 1)
-    last.then_inc(T.sem.mm, 1)
+        wt = T.wsb[:, TM * i:TM * (i + 1)]
+        p0 = g.tensor.matmul(T.acc0[:, 0:TH], wt, T["x%d" % i][:, 0:TH], k == 0, k == DEG - 1)
+        p1 = g.tensor.matmul(T.acc1[:, 0:TH], wt, T["x%d" % i][:, TH:TK], k == 0, k == DEG - 1)
+        if k == DEG - 1:
+            p0.then_inc(T.sem.m0, 1)
+            p1.then_inc(T.sem.m1, 1)
 
-    g.vector.wait_ge(T.sem.mm, 1)
-    g.vector.tensor_copy(T.ysb[:, :], T.acc[:, :]).then_inc(T.sem.cp, 1)
+    g.vector.wait_ge(T.sem.m0, 1)
+    g.vector.tensor_copy(T.ysb[:, 0:TH], T.acc0[:, 0:TH]).then_inc(T.sem.c0, 1)
+    g.scalar.wait_ge(T.sem.m1, 1)
+    g.scalar.activation(T.ysb[:, TH:TK], T.acc1[:, 0:TH], ActivationFunctionType.Copy).then_inc(T.sem.c1, 1)
 
-    g.sync.wait_ge(T.sem.cp, 1)
+    g.sync.wait_ge(T.sem.c0, 1)
+    g.sync.wait_ge(T.sem.c1, 1)
     g.sync.dma_start(T.y[:, :], T.ysb[:, :]).then_inc(T.sem.st, 16)
     g.sync.wait_ge(T.sem.st, 16)
     if sent:

from concourse.bass import DstId, RemoteDMATransfer
from concourse.mybir import ActivationFunctionType

N = 16
TK = 256
TH = TK // 2
TM = 128
DEG = 4

SCRATCH = {
    "x0": ("sbuf", [128, TK], "bfloat16"),
    "x1": ("sbuf", [128, TK], "bfloat16"),
    "x2": ("sbuf", [128, TK], "bfloat16"),
    "x3": ("sbuf", [128, TK], "bfloat16"),
    "hx": ("sbuf", [128, TK], "bfloat16"),
    "xd": ("dram", [128, TK], "bfloat16"),
    "wsb": ("sbuf", [128, DEG * TM], "bfloat16"),
    "ysb": ("sbuf", [128, TK], "bfloat16"),
    "acc0": ("psum", [128, 512], "float32"),
    "acc1": ("psum", [128, 512], "float32"),
}
SEMAPHORES = ["xl", "xs", "wl", "m0", "m1", "c0", "c1", "st", "sent"] + ["a%d" % j for j in range(N)]

ROUTES = {
    1: [(None, [("ports", 1, [7, 12, 13])]), (None, [("in", 1, [0])]), (8, [("in", 8, [0])])],
    2: [(None, [("off", 2, [11])]), (None, [("in", 2, [3])]), (13, [("all", 13, [3])])],
    3: [(None, [("ports", 3, [1, 7])])],
    4: [(None, [("off", 4, [5])]), (5, [("off", 5, [3])])],
    5: [(None, [("in", 5, [4])]), (None, [("off", 5, [7, 11, 15])])],
    6: [(None, [("ports", 6, [4, 8, 10, 14])])],
    7: [(None, [("ports", 7, [2, 10, 12])])],
    8: [(None, [("off", 8, [1, 4])]), (None, [("side", 8, [15, 12])])],
    9: [(None, [("off", 9, [6])]), (None, [("in", 9, [8])])],
    10: [(None, [("ports", 10, [2, 13])])],
    11: [(None, [("ports", 11, [5, 9])])],
    12: [(None, [("off", 12, [15, 0])]), (None, [("side", 12, [1, 9])]), (None, [("in", 12, [13])])],
    13: [(None, [("off", 13, [14, 2])]), (None, [("side", 13, [5, 8])])],
    14: [(None, [("off", 14, [6, 11])]), (13, [("off", 13, [10])])],
    15: [(None, [("ports", 15, [6, 4, 9])]), (12, [("in", 12, [14])])],
}


def _bits(m):
    return bin(m).count("1")


def make_plan(cores, topo):
    n = len(cores)

    def chip(r):
        return topo.chip(cores[r])

    calls = [[] for _ in range(n)]
    for r in range(n):
        for waited, trs in ROUTES.get(r, []):
            out = []
            for how, j, ds in trs:
                if how == "ports":
                    s = [d for d in ds if topo.same_plane(chip(r), chip(d))]
                    m = [d for d in ds if d not in s]
                    while len(m) > len(s) + 1:
                        s.append(m.pop())
                    while len(s) > len(m) + 1:
                        m.append(s.pop())
                    if m and s:
                        out += [("A", j, m), ("B", j, s)]
                    else:
                        out.append(("O", j, list(ds)))
                elif how == "side":
                    out += [("A", j, [ds[0]]), ("B", j, [ds[1]])]
                else:
                    out.append(({"off": "O", "in": "I", "all": "F"}[how], j, list(ds)))
            calls[r].append((waited, out))

    parts = {"O": "AB", "A": "A", "B": "B", "I": "I", "F": "ABI"}
    dur = {"O": 1.0, "A": 2.0, "B": 2.0, "I": 1.0, "F": 0.5}
    arrive = [{} for _ in range(n)]
    free = [{"A": 0.0, "B": 0.0, "I": 0.0} for _ in range(n)]
    at, clock = [0] * n, [0.0] * n
    moved = True
    while moved:
        moved = False
        for r in range(n):
            while at[r] < len(calls[r]):
                waited, trs = calls[r][at[r]]
                if waited is not None and waited not in arrive[r]:
                    break
                t0 = clock[r] + 0.3 if waited is None else max(clock[r] + 0.3, arrive[r][waited] + 2.0)
                clock[r] = t0
                for grp, j, ds in trs:
                    t = max([t0] + [free[r][p] for p in parts[grp]])
                    for d in ds:
                        t += dur[grp]
                        arrive[d][j] = t
                    for p in parts[grp]:
                        free[r][p] = t
                at[r] += 1
                moved = True
    return calls, arrive


def rank_program(g, core, T, topo):
    rank = T.rank_of(core)
    if rank is None:
        return
    cores, MASK = T.cores, T.tables["MASK"]
    calls, arrive = make_plan(cores, topo)

    def groups(c):
        full, low = 0, None
        for d in cores:
            if d != c:
                m = topo.mask(c, d)
                full |= m
                low = m if low is None else (low & m)
        bits = [b for b in range(full.bit_length()) if (low >> b) & 1]
        a = sum(1 << b for b in bits[:len(bits) // 2])
        return {"O": low, "A": a, "B": low & ~a, "I": full & ~low, "F": full}

    def slot(r, j):
        return T["x%d" % MASK[r].index(j)] if j in MASK[r] else T.hx

    need = {}
    for s in range(len(cores)):
        gs = groups(cores[s])
        for _, trs in calls[s]:
            for grp, j, ds in trs:
                if rank in ds:
                    need[j] = _bits(gs[grp])

    if calls[rank]:
        g.sync.dma_start(T.xd[:, :], T.x[:, :]).then_inc(T.sem.xl, 16)
    g.sync.dma_start(T.wsb[:, :], T.w[:, :]).then_inc(T.sem.wl, 16)
    g.sync.dma_start(slot(rank, rank)[:, :], T.x[:, :]).then_inc(T.sem.xs, 16)

    mine = groups(core)
    sent = 0
    if calls[rank]:
        g.wait_ge(T.sem.xl, 16)
    for waited, trs in calls[rank]:
        if waited is not None:
            g.wait_ge(T.sem["a%d" % waited], need[waited])
        lst = []
        for grp, j, ds in trs:
            ids = []
            for d in ds:
                rid, pid, _ = topo.addr(cores[d])
                ids.append(DstId(rid=rid, pnc=pid))
            src = T.xd if j == rank else slot(rank, j)
            lst.append(RemoteDMATransfer(dst_ids=ids, dma_engine_mask=mine[grp], remote_sem=T.sem["a%d" % j],
                                         srcs=[src[:, :]], dsts=[slot(d, j)[:, :] for d in ds], alu_op=0))
            sent += _bits(mine[grp])
        g.remote_dma_fused(lst, local_sem=T.sem.sent)

    order = sorted(range(DEG), key=lambda i: (arrive[rank].get(MASK[rank][i], 0.0), i))
    g.tensor.wait_ge(T.sem.wl, 16)
    for k, i in enumerate(order):
        j = MASK[rank][i]
        if j == rank:
            g.tensor.wait_ge(T.sem.xs, 16)
        else:
            g.tensor.wait_ge(T.sem["a%d" % j], need[j])
        wt = T.wsb[:, TM * i:TM * (i + 1)]
        p0 = g.tensor.matmul(T.acc0[:, 0:TH], wt, T["x%d" % i][:, 0:TH], k == 0, k == DEG - 1)
        p1 = g.tensor.matmul(T.acc1[:, 0:TH], wt, T["x%d" % i][:, TH:TK], k == 0, k == DEG - 1)
        if k == DEG - 1:
            p0.then_inc(T.sem.m0, 1)
            p1.then_inc(T.sem.m1, 1)

    g.vector.wait_ge(T.sem.m0, 1)
    g.vector.tensor_copy(T.ysb[:, 0:TH], T.acc0[:, 0:TH]).then_inc(T.sem.c0, 1)
    g.scalar.wait_ge(T.sem.m1, 1)
    g.scalar.activation(T.ysb[:, TH:TK], T.acc1[:, 0:TH], ActivationFunctionType.Copy).then_inc(T.sem.c1, 1)

    g.sync.wait_ge(T.sem.c0, 1)
    g.sync.wait_ge(T.sem.c1, 1)
    g.sync.dma_start(T.y[:, :], T.ysb[:, :]).then_inc(T.sem.st, 16)
    g.sync.wait_ge(T.sem.st, 16)
    if sent:
        g.wait_ge(T.sem.sent, sent)
